import numpy as np, ml_dtypes
CORES = [4,20,60,84,92,100,116]
N = 7
import mx_ref
NC = 256
def at(b): return (b, 0) if b < N else (2 * N - 1 - b, 1)
BF = ml_dtypes.bfloat16
def setup_inputs(rng):
    def f(*shape):
        return mx_ref.flush((rng.standard_normal(shape, dtype=np.float32) * np.exp2(rng.integers(-2, 3, shape[:-1] + (1,)))).astype(BF))
    return {"k": f(N, 128, 2 * 512), "q": f(N, 128, 2 * 4 * NC)}
def setup_inputs_blocks(rng):
    d = setup_inputs(rng)
    for k in ("k", "q"): d[k] = mx_ref.spread(d[k], rng, 4)
    return d
def setup_inputs_wide(rng):
    d = setup_inputs(rng)
    for k in ("k", "q"): d[k] = mx_ref.flush((d[k].astype(np.float32) * np.exp2(rng.integers(-8, 9, (N, 1, 1))).astype(np.float32)).astype(BF))
    return d
def setup_inputs_zeros(rng):
    d = setup_inputs(rng); v = d["q"].reshape(N, 128, -1, 4).copy()
    v[np.broadcast_to((rng.random((N, 1, v.shape[2], 1)) < 0.33), v.shape)] = 0
    d["q"] = v.reshape(d["q"].shape)
    return d
def reference(k, q):
    QK = [mx_ref.quantize(k[at(b)[0]][:, 512 * at(b)[1]:512 * at(b)[1] + 512]) for b in range(2 * N)]
    QQ = [mx_ref.quantize(q[at(b)[0]][:, 4 * NC * at(b)[1]:4 * NC * at(b)[1] + 4 * NC]) for b in range(2 * N)]
    y = np.zeros((N, 128, (2 * N + 1) * NC), np.float32)
    for r in range(N):
        c = 0
        for a in (r, 2 * N - 1 - r):
            for b in range(a + 1):
                y[r][:, c:c + NC] = mx_ref.matmul(QK[b], QQ[a]); c += NC
    return {"y": y}

from concourse.bass import DstId, RemoteDMATransfer
from concourse.mybir import dt, ActivationFunctionType

N = 7
KW = 128
QW = 256
NBLK = 2 * N + 1
BANKS = 8
BANK = 512

ND = 2
HCAP = 40
RELAY = 20
FAR_N = 8
NEAR_N = 8
FLUSH = (1, 1, 1, 1, 1, 1)

SCRATCH = {
    "kin": ("sbuf", [128, 2 * 4 * KW], "bfloat16"),
    "qin": ("sbuf", [128, 2 * 4 * QW], "bfloat16"),
    "kc": ("sbuf", [128, 2 * N * KW], "float8_e4m3fn_x4"),
    "ks": ("sbuf", [128, 2 * N * KW], "uint8"),
    "qc": ("sbuf", [128, 2 * QW], "float8_e4m3fn_x4"),
    "qs": ("sbuf", [128, 2 * QW], "uint8"),
    "ysb": ("sbuf", [128, NBLK * QW], "float32"),
    "ps": ("psum", [128, BANKS * BANK], "float32"),
}
SEMAPHORES = (["kld", "qld", "kq", "qq", "sent", "hp", "hc", "sta", "stb"]
              + ["arr%d" % s for s in range(N)]
              + ["mm%d" % i for i in range(NBLK)]
              + ["cp%d" % i for i in range(NBLK)])


def _width(s, d):
    return 2 if s > d else 1


def _parts(w):
    return 4 + w, 4 + 4 * w


def _cost(w):
    return sum(_parts(w))


def _plan(cores, topo):
    n = len(cores)
    every = range(topo.CORES_PER_CHIP * topo.CHIPS)
    port = {}

    def gate(c, d):
        return (topo.chip(cores[d]), topo.die(c), topo.mates(topo.chip(c), topo.chip(cores[d])))

    direct, groups = {}, []
    for s in range(n):
        turn = [(s - j) % n for j in range(1, n)]
        reach = [d for d in turn if topo.may_write(cores[s], cores[d])]
        subsets = [[]]
        for d in reach:
            subsets += [x + [d] for x in subsets]
        best = None
        for sub in subsets:
            if len(sub) != min(ND, len(reach)):
                continue
            grp = []
            for w in (2, 1):
                rest = [d for d in turn if d not in sub and _width(s, d) == w]
                if rest:
                    per = -(-len(rest) // -(-len(rest) * _cost(w) // HCAP))
                    grp += [(s, w, rest[a:a + per]) for a in range(0, len(rest), per)]
            top = max([sum(_cost(_width(s, d)) for d in sub)] + [len(ds) * _cost(w) for _s, w, ds in grp])
            key = (len(grp), top, [turn.index(d) for d in sub])
            if best is None or key < best[0]:
                best = (key, sub, grp)
        direct[s] = {w: [d for d in best[1] if _width(s, d) == w] for w in (2, 1)}
        for d in best[1]:
            port[gate(cores[s], d)] = port.get(gate(cores[s], d), 0) + _width(s, d)
        groups += best[2]
    groups.sort(key=lambda gr: -gr[1] * len(gr[2]))
    used = set(cores)
    helpers = {s: {2: [], 1: []} for s in range(n)}
    job = {}
    slot = {}
    for s, w, ds in groups:
        cand = [c for c in every if topo.chip(c) == topo.chip(cores[s]) and c not in used
                and all(topo.may_write(c, cores[d]) for d in ds)]
        h = min(cand, key=lambda c: (max(port.get(gate(c, d), 0) for d in ds), topo.die(c) != topo.die(cores[s]), c))
        used.add(h)
        turns = [ds[a:] + ds[:a] for a in range(len(ds))]
        ds = min(turns, key=lambda t: sum(slot.get((d, i), 0) for i, d in enumerate(t)))
        for i, d in enumerate(ds):
            slot[(d, i)] = slot.get((d, i), 0) + 1
            port[gate(h, d)] = port.get(gate(h, d), 0) + w
        helpers[s][w].append((h, ds))
        job[h] = (s, w, ds)
    when, first = {}, {}
    for s in range(n):
        first[s] = sorted((2, 1), key=lambda w: -sum(len(ds) * _cost(w) for _h, ds in helpers[s][w]))
        t = v = 0
        for w in first[s]:
            plane, codes = _parts(w)
            t += plane * len(direct[s][w])
            for d in direct[s][w]:
                t += codes
                when[(s, d)] = t
            got = []
            for _h, ds in helpers[s][w]:
                v += plane
                got.append(v)
            for (_h, ds), u in zip(helpers[s][w], got):
                v += codes
                u = max(u + RELAY + plane * len(ds), v + RELAY // 4)
                for d in ds:
                    u += codes
                    when[(s, d)] = u
    order = {d: sorted([s for s in range(n) if s != d], key=lambda s: (when[(s, d)], s)) for d in range(n)}
    return {"direct": direct, "helpers": helpers, "job": job, "order": order, "first": first, "port": port}


def _pick(mask, k):
    bits = [b for b in range(mask.bit_length()) if (mask >> b) & 1]
    step = len(bits) // k
    return sum(1 << b for b in bits[::step][:k])


def _far_all(core, cores, topo):
    m = 0
    for c in cores:
        if topo.chip(c) != topo.chip(core):
            m = topo.mask(core, c) if m == 0 else m & topo.mask(core, c)
    return m


def _view(T, s, w, part):
    a, b = 2 * s * KW, (2 * s + w) * KW
    return T.ks[:, a:b] if part == 0 else T.kc[:, a:b].bitcast(dt.uint8)


def _xfer(T, topo, s, w, part, dsts, mask, sem):
    ids = []
    for c in dsts:
        rid, pid, _ring = topo.addr(c)
        ids.append(DstId(rid=rid, pnc=pid))
    return RemoteDMATransfer(dst_ids=ids, dma_engine_mask=mask, remote_sem=sem,
                             srcs=[_view(T, s, w, part)], dsts=[_view(T, s, w, part) for _c in dsts])


def _helper(g, core, T, topo, cores, job):
    s, w, ds = job
    far = _pick(_far_all(core, cores, topo), FAR_N)
    for part, sem in enumerate((T.sem.hp, T.sem.hc)):
        g.wait_ge(sem, NEAR_N)
        g.remote_dma_fused([_xfer(T, topo, s, w, part, [cores[d] for d in ds], far, T.sem["arr%d" % s])],
                           local_sem=T.sem.sent)
    g.wait_ge(T.sem.sent, 2 * FAR_N)


def rank_program(g, core, T, topo):
    cores = list(T.cores)
    plan = _plan(cores, topo)
    r = T.rank_of(core)
    if r is None:
        if core in plan["job"]:
            _helper(g, core, T, topo, cores, plan["job"][core])
        return

    g.sync.dma_start(T.kin[:], T.k[:]).then_inc(T.sem.kld, 16)
    g.sync.dma_start(T.qin[:], T.q[:]).then_inc(T.sem.qld, 16)

    g.vector.wait_ge(T.sem.kld, 16)
    for t in range(2):
        a = (2 * r + t) * KW
        g.vector.quantize_mx(T.kc[:, a:a + KW], T.ks[:, a:a + KW], T.kin[:, 4 * KW * t:4 * KW * (t + 1)]).then_inc(T.sem.kq, 1)
    g.vector.wait_ge(T.sem.qld, 16)
    for t in range(2):
        a = t * QW
        g.vector.quantize_mx(T.qc[:, a:a + QW], T.qs[:, a:a + QW], T.qin[:, 4 * QW * t:4 * QW * (t + 1)]).then_inc(T.sem.qq, 1)

    away = _far_all(core, cores, topo)
    far = _pick(away, FAR_N)
    g.wait_ge(T.sem.kq, 2)
    sent = 0
    for w in plan["first"][r]:
        ds = [cores[d] for d in plan["direct"][r][w]]
        hs = [h for h, _ds in plan["helpers"][r][w]]
        for part in range(2):
            xs = []
            if ds:
                xs.append(_xfer(T, topo, r, w, part, ds, far, T.sem["arr%d" % r]))
                sent += FAR_N
            if hs:
                near = _pick(topo.mask(core, hs[0]) & ~away, NEAR_N)
                xs.append(_xfer(T, topo, r, w, part, hs, near, (T.sem.hp, T.sem.hc)[part]))
                sent += NEAR_N
            if xs:
                g.remote_dma_fused(xs, local_sem=T.sem.sent)

    work = [(r, 0, 0, r), (r, 0, 1, r + 1 + r), (r, 1, 1, 2 * N)]
    marks = [len(work)]
    left = list(FLUSH)
    for s in plan["order"][r]:
        if s < r:
            work += [(s, 0, 0, s), (s, 0, 1, r + 1 + s)]
        else:
            work += [(s, 0, 1, r + 1 + s), (s, 1, 1, r + 1 + 2 * N - 1 - s)]
        left[0] -= 1
        if left[0] == 0:
            left.pop(0)
            marks.append(len(work))
    g.tensor.wait_ge(T.sem.kq, 2)
    g.tensor.wait_ge(T.sem.qq, 2)
    seen = {r}
    count = {"sta": 0, "stb": 0}
    ready = {}
    for i, (s, t, j, blk) in enumerate(work):
        if s not in seen:
            seen.add(s)
            g.tensor.wait_ge(T.sem["arr%d" % s], 2 * FAR_N)
        if i >= BANKS:
            g.tensor.wait_ge(T.sem["cp%d" % (i - BANKS)], 1)
        a, b, p = (2 * s + t) * KW, j * QW, (i % BANKS) * BANK
        g.tensor.matmul_mx(T.ps[:, p:p + QW], T.kc[:, a:a + KW], T.ks[:, a:a + KW],
                           T.qc[:, b:b + QW], T.qs[:, b:b + QW], True, True).then_inc(T.sem["mm%d" % i], 1)
        out = T.ysb[:, blk * QW:(blk + 1) * QW]
        if i % 2 == 0:
            g.vector.wait_ge(T.sem["mm%d" % i], 1)
            g.vector.tensor_copy(out, T.ps[:, p:p + QW]).then_inc(T.sem["cp%d" % i], 1)
        else:
            g.scalar.wait_ge(T.sem["mm%d" % i], 1)
            g.scalar.activation(out, T.ps[:, p:p + QW], ActivationFunctionType.Copy).then_inc(T.sem["cp%d" % i], 1)
        ready[blk] = i
        if i + 1 in marks:
            blks = sorted(ready)
            while blks:
                run = [blks.pop(0)]
                while blks and blks[0] == run[-1] + 1:
                    run.append(blks.pop(0))
                mine = all(ready[x] % 2 == 1 for x in run)
                q, sem = (g.scalar, "stb") if mine else (g.sync, "sta")
                for x in run:
                    q.wait_ge(T.sem["cp%d" % ready[x]], 1)
                lo, hi = run[0] * QW, (run[-1] + 1) * QW
                q.dma_start(T.y[:, lo:hi], T.ysb[:, lo:hi]).then_inc(T.sem[sem], 16)
                count[sem] += 16
            ready = {}
    g.sync.wait_ge(T.sem.sta, count["sta"])
    g.scalar.wait_ge(T.sem.stb, count["stb"])
    g.wait_ge(T.sem.sent, sent)
